import numpy as np
import ml_dtypes


def mxq(x, axis, fmt="e4m3"):
    dtype, down = {"e4m3": (ml_dtypes.float8_e4m3fn, 7), "e5m2": (ml_dtypes.float8_e5m2, 14)}[fmt]
    v = np.moveaxis(np.asarray(x, np.float32).astype(ml_dtypes.bfloat16).astype(np.float64), axis, -1)
    blocks = v.reshape(v.shape[:-1] + (-1, 32))
    amax = np.abs(blocks).max(-1, keepdims=True)
    byte = np.maximum(np.where(amax > 0, np.frexp(amax)[1] - 1 + 127, 0) - down, 1)
    scale = np.exp2(byte - 127.0)
    codes = (blocks / scale).astype(np.float32).astype(dtype).astype(np.float64)
    return np.moveaxis((codes * scale).reshape(v.shape), -1, axis)


WIDE = False


def mx_kscale(k, group=512):
    if not WIDE:
        return np.ones(k)
    levels = np.array([18, -18])
    if group != 512:
        return np.exp2(np.random.permutation(np.resize(levels, k // group))).repeat(group)
    if k % 512:
        return np.exp2(np.random.permutation(np.resize(levels, k // 32))).repeat(32)
    a = np.empty((k // 512, 16))
    for p in range(k // 512):
        a[p, :8] = np.random.permutation(np.resize(levels, 8))
        for g in range(8):
            far = levels[np.abs(levels - a[p, g]) >= 10]
            a[p, g + 8] = far[np.random.randint(len(far))]
    return np.exp2(a.ravel()).repeat(32)


def f64(x):
    return np.asarray(x).astype(np.float64)


def softplus(v):
    return np.log(1.0 + np.exp(v))


def sigmoid(v):
    return 1.0 / (1.0 + np.exp(-v))


G, D, M, O, N = 4, 128, 128, 128, 512


def sgn(shape):
    return np.random.uniform(0.5, 2.0, shape) * np.where(np.random.standard_normal(shape) < 0, -1.0, 1.0)


def setup_inputs():
    n = np.random.standard_normal
    s_d = mx_kscale(D, 0)
    s_m = mx_kscale(M, 0)
    return {
        "x": (n((G, D, N)) * s_d[:, None]).astype(np.float32),
        "w1": (n((G, D, M)) / np.sqrt(D) / s_d[:, None]).astype(np.float32),
        "w2": (n((G, D, M)) / np.sqrt(D) / s_d[:, None]).astype(np.float32),
        "gn": (np.random.uniform(0.5, 2.0, (G, M, 1))).astype(np.float32),
        "hs": (sgn((G, M, 1)) * s_m[:, None]).astype(np.float32),
        "wo2": (n((G, M, O)) / np.sqrt(M) / s_m[:, None]).astype(np.float32),
        "res": (0.5 * n((G, O, N))).astype(np.float32),
    }


def reference(x, w1, w2, gn, hs, wo2, res):
    w1q = mxq(f64(w1), 1, "e4m3")
    xq = mxq(f64(x), 1, "e4m3")
    z1 = w1q.transpose(0, 2, 1) @ xq
    w2q = mxq(f64(w2), 1, "e4m3")
    z2 = w2q.transpose(0, 2, 1) @ xq
    sp = softplus(z1) * softplus(z2)
    h = np.log(sp * f64(gn) + 1.0) * sigmoid(z1 - z2)
    hh = h * f64(hs)
    wo2q = mxq(f64(wo2), 1, "e4m3")
    hhq = mxq(hh, 1, "e4m3")
    y0 = wo2q.transpose(0, 2, 1) @ hhq
    y = y0 + f64(res)
    return y

@@ -1,0 +1,244 @@
+from contextlib import ExitStack
+
+import concourse.mybir as mybir
+
+G, D, M, O, N = 4, 128, 128, 128, 512
+FLOPS = 2 * G * N * (2 * D * M + M * O)
+
+F32 = mybir.dt.float32
+BF16 = mybir.dt.bfloat16
+U32 = mybir.dt.uint32
+U8 = mybir.dt.uint8
+FP8X4 = mybir.dt.float8_e4m3fn_x4
+ACT = mybir.ActivationFunctionType
+ALU = mybir.AluOpType
+
+P = 128
+PACK = 4
+ROWS = P // G
+C = 128
+CHUNKS = N // C
+RUN = 4
+
+
+def tile_rows_fsoftprod_kernel(tc, x, w1, w2, gn, hs, wo2, res, out):
+    nc = tc.nc
+    with ExitStack() as ctx:
+        sb = ctx.enter_context(tc.tile_pool(name="sb", bufs=1))
+        ps = ctx.enter_context(tc.psum_pool(name="ps", bufs=1))
+        ctx.enter_context(tc.manual_schedule())
+
+        def new(name, shape, dtype):
+            return sb.tile(shape, dtype, name=name, align_bytes=64)
+
+        def rows_of(g):
+            return slice(ROWS * g, ROWS * (g + 1))
+
+        def load_k_first(name, src):
+            width = src.shape[2]
+            raw = new(name + "_raw", [P, PACK, width], F32)
+            nc.sync.dma_start(out=raw[:], in_=src.rearrange("g (p j) n -> (g p) j n", j=PACK))
+            return raw
+
+        def interleave(name, copy, raw):
+            width = raw.shape[2]
+            grouped = new(name + "_grouped", [P, width, PACK], BF16)
+            copy(
+                out=grouped[:].rearrange("p (c i) j -> p c j i", i=RUN),
+                in_=raw.rearrange("p j (c i) -> p c j i", i=RUN),
+            )
+            return grouped
+
+        def quantize(name, grouped):
+            width = grouped.shape[1]
+            codes = new(name + "_codes", [P, width], U32)
+            scales = new(name + "_scales", [P, width], U8)
+            nc.vector.quantize_mx(
+                out=codes[:].bitcast(FP8X4),
+                scales=scales[:],
+                in_=grouped[:].rearrange("p n j -> p (n j)"),
+            )
+            return codes, scales
+
+        def product(dst, g, weights, moving, col0):
+            r = rows_of(g)
+            cols = slice(col0, col0 + C)
+            nc.tensor.matmul_mx(
+                out=dst,
+                lhsT=weights[0][r, :].bitcast(FP8X4),
+                lhsT_scale=weights[1][r, :],
+                rhs=moving[0][r, cols].bitcast(FP8X4),
+                rhs_scale=moving[1][r, cols],
+                start=True,
+                stop=True,
+            )
+
+        x0_raw = load_k_first("x0", x[:, :, 0:C])
+        w1_raw = load_k_first("w1", w1)
+        w2_raw = load_k_first("w2", w2)
+        x1_raw = load_k_first("x1", x[:, :, C : 2 * C])
+        x23_raw = load_k_first("x23", x[:, :, 2 * C : N])
+        gain = new("gain", [P, G], F32)
+        hscale = new("hscale", [P, G], F32)
+        with nc.allow_non_contiguous_dma(reason="one value a partition"):
+            nc.sync.dma_start(out=hscale[:], in_=hs.rearrange("g m o -> m (g o)"))
+            nc.sync.dma_start(out=gain[:], in_=gn.rearrange("g m o -> m (g o)"))
+        wo_raw = load_k_first("wo", wo2)
+        residual = new("residual", [P, G, N], F32)
+        nc.sync.dma_start(out=residual[:], in_=res.rearrange("g o n -> o g n"))
+
+        banks = [[ps.tile([P, 4 * C], F32, name="bank%d_%d" % (g, b)) for b in range(2)] for g in range(G)]
+
+        def z_of(g, c):
+            base = (c // 2) * 2 * C
+            return banks[g][c % 2][:, base : base + 2 * C]
+
+        x0_g = interleave("x0", nc.vector.tensor_copy, x0_raw[:])
+        w1_g = interleave("w1", nc.scalar.copy, w1_raw[:])
+        xq0 = quantize("x0", x0_g)
+        w2_g = interleave("w2", nc.vector.tensor_copy, w2_raw[:])
+        w1q = quantize("w1", w1_g)
+        w2q = quantize("w2", w2_g)
+        x1_g = interleave("x1", nc.scalar.copy, x1_raw[:])
+
+        e = [new("e%d" % c, [P, G, 2 * C], F32) for c in range(CHUNKS)]
+        z2 = [new("z2_%d" % c, [P, G, C], F32) for c in range(CHUNKS)]
+        diff = [new("diff%d" % c, [P, G, C], F32) for c in range(CHUNKS)]
+        th = [new("th%d" % c, [P, G, C], F32) for c in range(CHUNKS)]
+
+        def first_products(c, xq, col0):
+            for g in range(G):
+                z = z_of(g, c)
+                product(z[:, 0:C], g, w1q, xq, col0)
+                product(z[:, C : 2 * C], g, w2q, xq, col0)
+
+        def exps(c):
+            for g in range(G):
+                nc.scalar.activation(out=e[c][:, g, :], in_=z_of(g, c), func=ACT.Exp)
+
+        def differences(c):
+            def sub(g):
+                nc.vector.tensor_tensor(out=diff[c][:, g, :], in0=z_of(g, c)[:, 0:C], in1=z2[c][:, g, :], op=ALU.subtract)
+
+            for g in range(G):
+                nc.vector.tensor_copy(out=z2[c][:, g, :], in_=z_of(g, c)[:, C : 2 * C])
+                if g > 0:
+                    sub(g - 1)
+            sub(G - 1)
+
+        def tanh(c):
+            nc.scalar.activation(out=th[c][:], in_=diff[c][:], func=ACT.Tanh, scale=0.5)
+
+        first_products(0, xq0, 0)
+        xq1 = quantize("x1", x1_g)
+        exps(0)
+        first_products(1, xq1, 0)
+        x23_g = interleave("x23", nc.vector.tensor_copy, x23_raw[:])
+        differences(0)
+        xq23 = quantize("x23", x23_g)
+        exps(1)
+        first_products(2, xq23, 0)
+        differences(1)
+        tanh(0)
+        exps(2)
+        first_products(3, xq23, C)
+        differences(2)
+        tanh(1)
+        exps(3)
+        differences(3)
+        tanh(2)
+        tanh(3)
+
+        half = new("half", [P, G], F32)
+        nc.vector.tensor_scalar(out=half[:], in0=hscale[:], scalar1=0.5, scalar2=None, op0=ALU.mult)
+        wo_g = interleave("wo", nc.vector.tensor_copy, wo_raw[:])
+        gate = [new("gate%d" % c, [P, G, C], F32) for c in range(CHUNKS)]
+
+        def gates(c):
+            for g in range(G):
+                nc.vector.tensor_scalar(
+                    out=gate[c][:, g, :], in0=th[c][:, g, :], scalar1=1.0, scalar2=half[:, g : g + 1],
+                    op0=ALU.add, op1=ALU.mult,
+                )
+
+        gates(0)
+        woq = quantize("wo", wo_g)
+        for c in range(1, CHUNKS):
+            gates(c)
+
+        soft = [new("soft%d" % c, [P, G, 2 * C], F32) for c in range(CHUNKS)]
+        prod = [new("prod%d" % c, [P, G, C], F32) for c in range(CHUNKS)]
+        logp = [new("logp%d" % c, [P, G, C], F32) for c in range(CHUNKS)]
+        hh = [new("hh%d" % c, [P, G, C], BF16) for c in range(CHUNKS)]
+        moved = [new("moved%d" % c, [P, PACK, C], BF16) for c in range(CHUNKS)]
+        result = new("result", [P, G, N], F32)
+
+        def softplus(c):
+            nc.scalar.activation(out=soft[c][:], in_=e[c][:], func=ACT.Ln, bias=1.0)
+
+        def products(c):
+            for g in range(G):
+                nc.vector.scalar_tensor_tensor(
+                    out=prod[c][:, g, :], in0=soft[c][:, g, 0:C], scalar=gain[:, g : g + 1],
+                    in1=soft[c][:, g, C : 2 * C], op0=ALU.mult, op1=ALU.mult,
+                )
+
+        def logs(c, step):
+            for g in range(0, G, step):
+                nc.scalar.activation(out=logp[c][:, g : g + step, :], in_=prod[c][:, g : g + step, :], func=ACT.Ln, bias=1.0)
+
+        def hidden(c, step):
+            for g in range(0, G, step):
+                gs = slice(g, g + step)
+                nc.vector.tensor_tensor(out=hh[c][:, gs, :], in0=logp[c][:, gs, :], in1=gate[c][:, gs, :], op=ALU.mult)
+                for k in range(g, g + step):
+                    nc.sync.dma_start(out=moved[c][rows_of(k), :, :], in_=hh[c][:, k, :])
+
+        y_place = [(0, 0), (0, C), (1, 0), (0, 2 * C)]
+
+        def second_products(c, hq):
+            b, col = y_place[c]
+            for g in range(G):
+                product(banks[g][b][:, col : col + C], g, woq, hq, 0)
+
+        def finish(c0, c1, stores):
+            b, col = y_place[c0]
+            width = (c1 - c0) * C
+            cols = slice(c0 * C, c1 * C)
+            step = G // stores
+            for g in range(G):
+                nc.vector.tensor_tensor(
+                    out=result[:, g, cols], in0=banks[g][b][:, col : col + width], in1=residual[:, g, cols], op=ALU.add
+                )
+                if (g + 1) % step == 0:
+                    gs = slice(g + 1 - step, g + 1)
+                    nc.sync.dma_start(out=out[gs, :, cols].rearrange("g o n -> o g n"), in_=result[:, gs, cols])
+
+        softplus(0)
+        softplus(1)
+        products(0)
+        logs(0, G)
+        products(1)
+        softplus(2)
+        hidden(0, G)
+        logs(1, G)
+        products(2)
+        softplus(3)
+        hidden(1, G)
+        logs(2, G)
+        products(3)
+        hidden(2, G)
+        logs(3, 2)
+        hidden(3, 2)
+
+        h0 = interleave("h0", nc.scalar.copy, moved[0][:])
+        h1 = interleave("h1", nc.scalar.copy, moved[1][:])
+        second_products(0, quantize("h0", h0))
+        second_products(1, quantize("h1", h1))
+        h2 = interleave("h2", nc.scalar.copy, moved[2][:])
+        finish(0, 2, 1)
+        second_products(2, quantize("h2", h2))
+        h3 = interleave("h3", nc.vector.tensor_copy, moved[3][:])
+        finish(2, 3, 1)
+        second_products(3, quantize("h3", h3))
+        finish(3, 4, 2)

@@ -73,172 +73,228 @@ def tile_rows_fsoftprod_kernel(tc, x, w1, w2, gn, hs, wo2, res, out):
                 stop=True,
             )
 
-        x0_raw = load_k_first("x0", x[:, :, 0:C])
+        x_raw = [load_k_first("x0", x[:, :, 0:C])]
         w1_raw = load_k_first("w1", w1)
         w2_raw = load_k_first("w2", w2)
-        x1_raw = load_k_first("x1", x[:, :, C : 2 * C])
-        x23_raw = load_k_first("x23", x[:, :, 2 * C : N])
+        for c in range(1, CHUNKS):
+            x_raw.append(load_k_first("x%d" % c, x[:, :, c * C : (c + 1) * C]))
         gain = new("gain", [P, G], F32)
         hscale = new("hscale", [P, G], F32)
+        wo_raw = load_k_first("wo", wo2)
         with nc.allow_non_contiguous_dma(reason="one value a partition"):
             nc.sync.dma_start(out=hscale[:], in_=hs.rearrange("g m o -> m (g o)"))
             nc.sync.dma_start(out=gain[:], in_=gn.rearrange("g m o -> m (g o)"))
-        wo_raw = load_k_first("wo", wo2)
         residual = new("residual", [P, G, N], F32)
         nc.sync.dma_start(out=residual[:], in_=res.rearrange("g o n -> o g n"))
 
         banks = [[ps.tile([P, 4 * C], F32, name="bank%d_%d" % (g, b)) for b in range(2)] for g in range(G)]
 
         def z_of(g, c):
-            base = (c // 2) * 2 * C
-            return banks[g][c % 2][:, base : base + 2 * C]
-
-        x0_g = interleave("x0", nc.vector.tensor_copy, x0_raw[:])
-        w1_g = interleave("w1", nc.scalar.copy, w1_raw[:])
-        xq0 = quantize("x0", x0_g)
-        w2_g = interleave("w2", nc.vector.tensor_copy, w2_raw[:])
-        w1q = quantize("w1", w1_g)
-        w2q = quantize("w2", w2_g)
-        x1_g = interleave("x1", nc.scalar.copy, x1_raw[:])
+            b, col = [(0, 0), (1, 0), (1, 2 * C), (0, 2 * C)][c]
+            return banks[g][b][:, col : col + 2 * C]
 
         e = [new("e%d" % c, [P, G, 2 * C], F32) for c in range(CHUNKS)]
-        z2 = [new("z2_%d" % c, [P, G, C], F32) for c in range(CHUNKS)]
-        diff = [new("diff%d" % c, [P, G, C], F32) for c in range(CHUNKS)]
-        th = [new("th%d" % c, [P, G, C], F32) for c in range(CHUNKS)]
+        spans = [(0, 1), (1, 3), (3, 4)]
+        z2 = [new("z2_%d" % u, [P, G, c1 - c0, C], F32) for u, (c0, c1) in enumerate(spans)]
+        diff = [new("diff%d" % u, [P, G, c1 - c0, C], F32) for u, (c0, c1) in enumerate(spans)]
+        th = new("th", [P, G, N], F32)
 
-        def first_products(c, xq, col0):
+        def z_span(u, g):
+            if u == 1:
+                return banks[g][1][:].rearrange("p (c n) -> p c n", n=2 * C)
+            return z_of(g, spans[u][0]).rearrange("p (c n) -> p c n", n=2 * C)
+
+        def first_products(c, xq):
             for g in range(G):
                 z = z_of(g, c)
-                product(z[:, 0:C], g, w1q, xq, col0)
-                product(z[:, C : 2 * C], g, w2q, xq, col0)
+                product(z[:, 0:C], g, w1q, xq, 0)
+                product(z[:, C : 2 * C], g, w2q, xq, 0)
 
-        def exps(c):
+        def exps(c, lo, hi):
             for g in range(G):
-                nc.scalar.activation(out=e[c][:, g, :], in_=z_of(g, c), func=ACT.Exp)
+                nc.scalar.activation(out=e[c][:, g, lo:hi], in_=z_of(g, c)[:, lo:hi], func=ACT.Exp)
 
-        def differences(c):
-            def sub(g):
-                nc.vector.tensor_tensor(out=diff[c][:, g, :], in0=z_of(g, c)[:, 0:C], in1=z2[c][:, g, :], op=ALU.subtract)
+        def copy_z2(u, g):
+            nc.vector.tensor_copy(out=z2[u][:, g], in_=z_span(u, g)[:, :, C : 2 * C])
 
-            for g in range(G):
-                nc.vector.tensor_copy(out=z2[c][:, g, :], in_=z_of(g, c)[:, C : 2 * C])
-                if g > 0:
-                    sub(g - 1)
-            sub(G - 1)
+        def subtract(u, g):
+            nc.vector.tensor_tensor(out=diff[u][:, g], in0=z_span(u, g)[:, :, 0:C], in1=z2[u][:, g], op=ALU.subtract)
 
-        def tanh(c):
-            nc.scalar.activation(out=th[c][:], in_=diff[c][:], func=ACT.Tanh, scale=0.5)
+        def tanh(u, g0, g1):
+            c0, c1 = spans[u]
+            nc.scalar.activation(
+                out=th[:, g0:g1, c0 * C : c1 * C],
+                in_=diff[u][:, g0:g1].rearrange("p g c n -> p g (c n)"),
+                func=ACT.Tanh,
+                scale=0.5,
+            )
 
-        first_products(0, xq0, 0)
-        xq1 = quantize("x1", x1_g)
-        exps(0)
-        first_products(1, xq1, 0)
-        x23_g = interleave("x23", nc.vector.tensor_copy, x23_raw[:])
-        differences(0)
-        xq23 = quantize("x23", x23_g)
-        exps(1)
-        first_products(2, xq23, 0)
-        differences(1)
-        tanh(0)
-        exps(2)
-        first_products(3, xq23, C)
-        differences(2)
-        tanh(1)
-        exps(3)
-        differences(3)
-        tanh(2)
-        tanh(3)
+        x0_g = interleave("x0", nc.vector.tensor_copy, x_raw[0][:])
+        w1_g = interleave("w1", nc.vector.tensor_copy, w1_raw[:])
+        xq0 = quantize("x0", x0_g)
+        w1q = quantize("w1", w1_g)
+        for g in range(G):
+            product(z_of(g, 0)[:, 0:C], g, w1q, xq0, 0)
+        w2_g = interleave("w2", nc.vector.tensor_copy, w2_raw[:])
+        exps(0, 0, C)
+        w2q = quantize("w2", w2_g)
+        for g in range(G):
+            product(z_of(g, 0)[:, C : 2 * C], g, w2q, xq0, 0)
+        x1_g = interleave("x1", nc.vector.tensor_copy, x_raw[1][:])
+        exps(0, C, 2 * C)
+        first_products(1, quantize("x1", x1_g))
+        x2_g = interleave("x2", nc.vector.tensor_copy, x_raw[2][:])
+        exps(1, 0, 2 * C)
+        copy_z2(0, 0)
+        first_products(2, quantize("x2", x2_g))
+        exps(2, 0, 2 * C)
+        copy_z2(0, 1)
+        subtract(0, 0)
+        x3_g = interleave("x3", nc.vector.tensor_copy, x_raw[3][:])
+        copy_z2(0, 2)
+        subtract(0, 1)
+        copy_z2(0, 3)
+        xq3 = quantize("x3", x3_g)
+        subtract(0, 2)
+        subtract(0, 3)
+        tanh(0, 0, G)
+        first_products(3, xq3)
+        exps(3, 0, 2 * C)
+        units = [(u, g) for u in (1, 2) for g in range(G)]
+        copy_z2(*units[0])
+        copy_z2(*units[1])
+        for k, (u, g) in enumerate(units):
+            subtract(u, g)
+            if u == 1 and g % 2 == 1:
+                tanh(1, g - 1, g + 1)
+            if k + 2 < len(units):
+                copy_z2(*units[k + 2])
+        tanh(2, 0, 3)
+        tanh(2, 3, G)
 
         half = new("half", [P, G], F32)
         nc.vector.tensor_scalar(out=half[:], in0=hscale[:], scalar1=0.5, scalar2=None, op0=ALU.mult)
         wo_g = interleave("wo", nc.vector.tensor_copy, wo_raw[:])
-        gate = [new("gate%d" % c, [P, G, C], F32) for c in range(CHUNKS)]
-
-        def gates(c):
-            for g in range(G):
-                nc.vector.tensor_scalar(
-                    out=gate[c][:, g, :], in0=th[c][:, g, :], scalar1=1.0, scalar2=half[:, g : g + 1],
-                    op0=ALU.add, op1=ALU.mult,
-                )
-
-        gates(0)
-        woq = quantize("wo", wo_g)
-        for c in range(1, CHUNKS):
-            gates(c)
+        gate = new("gate", [P, G, N], F32)
+        for g in range(G):
+            nc.vector.tensor_scalar(
+                out=gate[:, g, :], in0=th[:, g, :], scalar1=1.0, scalar2=half[:, g : g + 1],
+                op0=ALU.add, op1=ALU.mult,
+            )
+            if g == 0:
+                woq = quantize("wo", wo_g)
 
         soft = [new("soft%d" % c, [P, G, 2 * C], F32) for c in range(CHUNKS)]
         prod = [new("prod%d" % c, [P, G, C], F32) for c in range(CHUNKS)]
         logp = [new("logp%d" % c, [P, G, C], F32) for c in range(CHUNKS)]
         hh = [new("hh%d" % c, [P, G, C], BF16) for c in range(CHUNKS)]
         moved = [new("moved%d" % c, [P, PACK, C], BF16) for c in range(CHUNKS)]
-        result = new("result", [P, G, N], F32)
+        result = [new("result%d" % c, [P, G, C], F32) for c in range(CHUNKS)]
 
-        def softplus(c):
-            nc.scalar.activation(out=soft[c][:], in_=e[c][:], func=ACT.Ln, bias=1.0)
+        parts = [(c, slice(g, g + 2)) for c in range(CHUNKS) for g in (0, 2)][:-1]
+        parts = parts + [(CHUNKS - 1, slice(g, g + 1)) for g in (2, 3)]
 
-        def products(c):
-            for g in range(G):
+        def part(k):
+            return parts[k]
+
+        def softplus(k):
+            c, gs = part(k)
+            nc.scalar.activation(out=soft[c][:, gs, :], in_=e[c][:, gs, :], func=ACT.Ln, bias=1.0)
+
+        def products(k):
+            c, gs = part(k)
+            for g in range(gs.start, gs.stop):
                 nc.vector.scalar_tensor_tensor(
                     out=prod[c][:, g, :], in0=soft[c][:, g, 0:C], scalar=gain[:, g : g + 1],
                     in1=soft[c][:, g, C : 2 * C], op0=ALU.mult, op1=ALU.mult,
                 )
 
-        def logs(c, step):
-            for g in range(0, G, step):
-                nc.scalar.activation(out=logp[c][:, g : g + step, :], in_=prod[c][:, g : g + step, :], func=ACT.Ln, bias=1.0)
+        def logs(k):
+            c, gs = part(k)
+            nc.scalar.activation(out=logp[c][:, gs, :], in_=prod[c][:, gs, :], func=ACT.Ln, bias=1.0)
 
-        def hidden(c, step):
-            for g in range(0, G, step):
-                gs = slice(g, g + step)
-                nc.vector.tensor_tensor(out=hh[c][:, gs, :], in0=logp[c][:, gs, :], in1=gate[c][:, gs, :], op=ALU.mult)
-                for k in range(g, g + step):
-                    nc.sync.dma_start(out=moved[c][rows_of(k), :, :], in_=hh[c][:, k, :])
+        def hidden(k):
+            c, gs = part(k)
+            nc.vector.tensor_tensor(
+                out=hh[c][:, gs, :], in0=logp[c][:, gs, :], in1=gate[:, gs, c * C : (c + 1) * C], op=ALU.mult
+            )
+            for g in range(gs.start, gs.stop):
+                nc.sync.dma_start(out=moved[c][rows_of(g), :, :], in_=hh[c][:, g, :])
 
-        y_place = [(0, 0), (0, C), (1, 0), (0, 2 * C)]
+        def y_of(g, c):
+            return banks[g][c % 2][:, 0:C]
 
-        def second_products(c, hq):
-            b, col = y_place[c]
+        def second_products(c, grouped):
+            hq = quantize("h%d" % c, grouped)
             for g in range(G):
-                product(banks[g][b][:, col : col + C], g, woq, hq, 0)
+                product(y_of(g, c), g, woq, hq, 0)
 
-        def finish(c0, c1, stores):
-            b, col = y_place[c0]
-            width = (c1 - c0) * C
-            cols = slice(c0 * C, c1 * C)
-            step = G // stores
-            for g in range(G):
-                nc.vector.tensor_tensor(
-                    out=result[:, g, cols], in0=banks[g][b][:, col : col + width], in1=residual[:, g, cols], op=ALU.add
+        def finish(c, g0, g1, store_from):
+            cols = slice(c * C, (c + 1) * C)
+            for g in range(g0, g1):
+                nc.vector.tensor_tensor(out=result[c][:, g, :], in0=y_of(g, c), in1=residual[:, g, cols], op=ALU.add)
+            if store_from is not None:
+                gs = slice(store_from, g1)
+                nc.sync.dma_start(out=out[gs, :, cols].rearrange("g o n -> o g n"), in_=result[c][:, gs, :])
+
+        def interleave_shared(name, raw, split):
+            grouped = new(name + "_grouped", [P, C, PACK], BF16)
+            for copy, cols in ((nc.scalar.copy, slice(0, split)), (nc.vector.tensor_copy, slice(split, C))):
+                copy(
+                    out=grouped[:, cols, :].rearrange("p (c i) j -> p c j i", i=RUN),
+                    in_=raw[:, :, cols].rearrange("p j (c i) -> p c j i", i=RUN),
                 )
-                if (g + 1) % step == 0:
-                    gs = slice(g + 1 - step, g + 1)
-                    nc.sync.dma_start(out=out[gs, :, cols].rearrange("g o n -> o g n"), in_=result[:, gs, cols])
+            return grouped
 
         softplus(0)
-        softplus(1)
         products(0)
-        logs(0, G)
+        softplus(1)
         products(1)
+        logs(0)
+        hidden(0)
         softplus(2)
-        hidden(0, G)
-        logs(1, G)
         products(2)
+        logs(1)
+        hidden(1)
         softplus(3)
-        hidden(1, G)
-        logs(2, G)
         products(3)
-        hidden(2, G)
-        logs(3, 2)
-        hidden(3, 2)
-
-        h0 = interleave("h0", nc.scalar.copy, moved[0][:])
+        logs(2)
+        hidden(2)
+        softplus(4)
+        products(4)
+        logs(3)
+        hidden(3)
+        softplus(5)
+        products(5)
+        logs(4)
+        hidden(4)
+        softplus(6)
+        h0 = interleave("h0", nc.vector.tensor_copy, moved[0][:])
+        products(6)
+        softplus(7)
+        products(7)
+        logs(5)
+        softplus(8)
+        hidden(5)
+        products(8)
+        logs(6)
+        second_products(0, h0)
+        hidden(6)
+        logs(7)
+        hidden(7)
+        logs(8)
+        hidden(8)
         h1 = interleave("h1", nc.scalar.copy, moved[1][:])
-        second_products(0, quantize("h0", h0))
-        second_products(1, quantize("h1", h1))
-        h2 = interleave("h2", nc.scalar.copy, moved[2][:])
-        finish(0, 2, 1)
-        second_products(2, quantize("h2", h2))
-        h3 = interleave("h3", nc.vector.tensor_copy, moved[3][:])
-        finish(2, 3, 1)
-        second_products(3, quantize("h3", h3))
-        finish(3, 4, 2)
+        finish(0, 0, 2, None)
+        second_products(1, h1)
+        finish(0, 2, G, 0)
+        finish(1, 0, 2, None)
+        h2 = interleave("h2", nc.vector.tensor_copy, moved[2][:])
+        finish(1, 2, G, 0)
+        second_products(2, h2)
+        h3 = interleave_shared("h3", moved[3], 48)
+        second_products(3, h3)
+        finish(2, 0, 2, 0)
+        finish(2, 2, G, 2)
+        finish(3, 0, 2, 0)
+        finish(3, 2, G, 2)

@@ -18,7 +18,9 @@ PACK = 4
 ROWS = P // G
 C = 128
 CHUNKS = N // C
+LAST = CHUNKS - 1
 RUN = 4
+SCALAR_COLS = 48
 
 
 def tile_rows_fsoftprod_kernel(tc, x, w1, w2, gn, hs, wo2, res, out):
@@ -34,25 +36,30 @@ def tile_rows_fsoftprod_kernel(tc, x, w1, w2, gn, hs, wo2, res, out):
         def rows_of(g):
             return slice(ROWS * g, ROWS * (g + 1))
 
-        def load_k_first(name, src):
-            width = src.shape[2]
-            raw = new(name + "_raw", [P, PACK, width], F32)
+        def load_by_row_tile(name, src):
+            raw = new(name, [P, PACK, src.shape[2]], F32)
             nc.sync.dma_start(out=raw[:], in_=src.rearrange("g (p j) n -> (g p) j n", j=PACK))
             return raw
 
-        def interleave(name, copy, raw):
-            width = raw.shape[2]
-            grouped = new(name + "_grouped", [P, width, PACK], BF16)
-            copy(
-                out=grouped[:].rearrange("p (c i) j -> p c j i", i=RUN),
-                in_=raw.rearrange("p j (c i) -> p c j i", i=RUN),
-            )
+        def move_to_row_tile(dst, src, g):
+            nc.sync.dma_start(out=dst[rows_of(g), :, :], in_=src[:, g, :])
+
+        def interleave(name, raw, shares):
+            grouped = new(name, [P, C, PACK], BF16)
+            for copy, cols in shares:
+                copy(
+                    out=grouped[:, cols, :].rearrange("p (c i) j -> p c j i", i=RUN),
+                    in_=raw[:, :, cols].rearrange("p j (c i) -> p c j i", i=RUN),
+                )
             return grouped
 
+        on_vector = [(nc.vector.tensor_copy, slice(0, C))]
+        on_scalar = [(nc.scalar.copy, slice(0, C))]
+        on_both = [(nc.scalar.copy, slice(0, SCALAR_COLS)), (nc.vector.tensor_copy, slice(SCALAR_COLS, C))]
+
         def quantize(name, grouped):
-            width = grouped.shape[1]
-            codes = new(name + "_codes", [P, width], U32)
-            scales = new(name + "_scales", [P, width], U8)
+            codes = new(name + "_codes", [P, C], U32)
+            scales = new(name + "_scales", [P, C], U8)
             nc.vector.quantize_mx(
                 out=codes[:].bitcast(FP8X4),
                 scales=scales[:],
@@ -60,97 +67,96 @@ def tile_rows_fsoftprod_kernel(tc, x, w1, w2, gn, hs, wo2, res, out):
             )
             return codes, scales
 
-        def product(dst, g, weights, moving, col0):
+        def product(dst, g, weights, moving):
             r = rows_of(g)
-            cols = slice(col0, col0 + C)
             nc.tensor.matmul_mx(
                 out=dst,
                 lhsT=weights[0][r, :].bitcast(FP8X4),
                 lhsT_scale=weights[1][r, :],
-                rhs=moving[0][r, cols].bitcast(FP8X4),
-                rhs_scale=moving[1][r, cols],
+                rhs=moving[0][r, :].bitcast(FP8X4),
+                rhs_scale=moving[1][r, :],
                 start=True,
                 stop=True,
             )
 
-        x_raw = [load_k_first("x0", x[:, :, 0:C])]
-        w1_raw = load_k_first("w1", w1)
-        w2_raw = load_k_first("w2", w2)
+        x_raw = [load_by_row_tile("x0_raw", x[:, :, 0:C])]
+        w1_raw = load_by_row_tile("w1_raw", w1)
+        w2_raw = load_by_row_tile("w2_raw", w2)
         for c in range(1, CHUNKS):
-            x_raw.append(load_k_first("x%d" % c, x[:, :, c * C : (c + 1) * C]))
-        gain = new("gain", [P, G], F32)
+            x_raw.append(load_by_row_tile("x%d_raw" % c, x[:, :, c * C : (c + 1) * C]))
+        wo_raw = load_by_row_tile("wo_raw", wo2)
         hscale = new("hscale", [P, G], F32)
-        wo_raw = load_k_first("wo", wo2)
-        with nc.allow_non_contiguous_dma(reason="one value a partition"):
+        gain = new("gain", [P, G], F32)
+        with nc.allow_non_contiguous_dma(reason="one value for each partition and group"):
             nc.sync.dma_start(out=hscale[:], in_=hs.rearrange("g m o -> m (g o)"))
             nc.sync.dma_start(out=gain[:], in_=gn.rearrange("g m o -> m (g o)"))
+        gain_rt = new("gain_rt", [P, PACK], F32)
+        nc.sync.dma_start(out=gain_rt[:], in_=gn.rearrange("g (p j) o -> (g p) (j o)", j=PACK))
         residual = new("residual", [P, G, N], F32)
         nc.sync.dma_start(out=residual[:], in_=res.rearrange("g o n -> o g n"))
 
         banks = [[ps.tile([P, 4 * C], F32, name="bank%d_%d" % (g, b)) for b in range(2)] for g in range(G)]
 
-        def z_of(g, c):
-            b, col = [(0, 0), (1, 0), (1, 2 * C), (0, 2 * C)][c]
-            return banks[g][b][:, col : col + 2 * C]
+        def bank_of(g, c):
+            return banks[g][1 if 0 < c < LAST else 0]
 
-        e = [new("e%d" % c, [P, G, 2 * C], F32) for c in range(CHUNKS)]
-        spans = [(0, 1), (1, 3), (3, 4)]
-        z2 = [new("z2_%d" % u, [P, G, c1 - c0, C], F32) for u, (c0, c1) in enumerate(spans)]
-        diff = [new("diff%d" % u, [P, G, c1 - c0, C], F32) for u, (c0, c1) in enumerate(spans)]
-        th = new("th", [P, G, N], F32)
+        spans = [(0, 1), (1, LAST), (LAST, CHUNKS)]
 
-        def z_span(u, g):
-            if u == 1:
-                return banks[g][1][:].rearrange("p (c n) -> p c n", n=2 * C)
-            return z_of(g, spans[u][0]).rearrange("p (c n) -> p c n", n=2 * C)
+        def z_of(g, c0, c1):
+            col = (c0 // 2) * 2 * C
+            return bank_of(g, c0)[:, col : col + (c1 - c0) * 2 * C].rearrange("p (c n) -> p c n", n=2 * C)
 
-        def first_products(c, xq):
+        exp_z = [new("exp_z%d" % c, [P, G, 2 * C], F32) for c in range(CHUNKS)]
+        z2 = [new("z2_%d" % s, [P, G, c1 - c0, C], F32) for s, (c0, c1) in enumerate(spans)]
+        diff = [new("diff%d" % s, [P, G, c1 - c0, C], F32) for s, (c0, c1) in enumerate(spans)]
+        tanh_half = [new("tanh_half%d" % s, [P, G, (c1 - c0) * C], F32) for s, (c0, c1) in enumerate(spans)]
+        Z1, Z2, BOTH = slice(0, C), slice(C, 2 * C), slice(0, 2 * C)
+
+        def first_products(c, xq, which):
             for g in range(G):
-                z = z_of(g, c)
-                product(z[:, 0:C], g, w1q, xq, 0)
-                product(z[:, C : 2 * C], g, w2q, xq, 0)
+                for weights, cols in which:
+                    product(z_of(g, c, c + 1)[:, 0, cols], g, weights, xq)
 
-        def exps(c, lo, hi):
+        def exps(c, cols):
             for g in range(G):
-                nc.scalar.activation(out=e[c][:, g, lo:hi], in_=z_of(g, c)[:, lo:hi], func=ACT.Exp)
+                nc.scalar.activation(out=exp_z[c][:, g, cols], in_=z_of(g, c, c + 1)[:, 0, cols], func=ACT.Exp)
 
-        def copy_z2(u, g):
-            nc.vector.tensor_copy(out=z2[u][:, g], in_=z_span(u, g)[:, :, C : 2 * C])
+        def copy_z2(s, g):
+            nc.vector.tensor_copy(out=z2[s][:, g], in_=z_of(g, *spans[s])[:, :, Z2])
 
-        def subtract(u, g):
-            nc.vector.tensor_tensor(out=diff[u][:, g], in0=z_span(u, g)[:, :, 0:C], in1=z2[u][:, g], op=ALU.subtract)
+        def subtract(s, g):
+            nc.vector.tensor_tensor(out=diff[s][:, g], in0=z_of(g, *spans[s])[:, :, Z1], in1=z2[s][:, g], op=ALU.subtract)
 
-        def tanh(u, g0, g1):
-            c0, c1 = spans[u]
+        def tanh(s, g0, g1):
             nc.scalar.activation(
-                out=th[:, g0:g1, c0 * C : c1 * C],
-                in_=diff[u][:, g0:g1].rearrange("p g c n -> p g (c n)"),
+                out=tanh_half[s][:, g0:g1, :],
+                in_=diff[s][:, g0:g1].rearrange("p g c n -> p g (c n)"),
                 func=ACT.Tanh,
                 scale=0.5,
             )
 
-        x0_g = interleave("x0", nc.vector.tensor_copy, x_raw[0][:])
-        w1_g = interleave("w1", nc.vector.tensor_copy, w1_raw[:])
+        x0_g = interleave("x0_g", x_raw[0], on_vector)
+        w1_g = interleave("w1_g", w1_raw, on_both)
         xq0 = quantize("x0", x0_g)
         w1q = quantize("w1", w1_g)
-        for g in range(G):
-            product(z_of(g, 0)[:, 0:C], g, w1q, xq0, 0)
-        w2_g = interleave("w2", nc.vector.tensor_copy, w2_raw[:])
-        exps(0, 0, C)
+        first_products(0, xq0, [(w1q, Z1)])
+        w2_g = interleave("w2_g", w2_raw, on_both)
+        exps(0, Z1)
         w2q = quantize("w2", w2_g)
-        for g in range(G):
-            product(z_of(g, 0)[:, C : 2 * C], g, w2q, xq0, 0)
-        x1_g = interleave("x1", nc.vector.tensor_copy, x_raw[1][:])
-        exps(0, C, 2 * C)
-        first_products(1, quantize("x1", x1_g))
-        x2_g = interleave("x2", nc.vector.tensor_copy, x_raw[2][:])
-        exps(1, 0, 2 * C)
+        first_products(0, xq0, [(w2q, Z2)])
+        both_weights = [(w1q, Z1), (w2q, Z2)]
+        x1_g = interleave("x1_g", x_raw[1], on_vector)
+        exps(0, Z2)
+        first_products(1, quantize("x1", x1_g), both_weights)
+
+        x2_g = interleave("x2_g", x_raw[2], on_vector)
+        exps(1, BOTH)
         copy_z2(0, 0)
-        first_products(2, quantize("x2", x2_g))
-        exps(2, 0, 2 * C)
+        first_products(2, quantize("x2", x2_g), both_weights)
+        exps(2, BOTH)
         copy_z2(0, 1)
         subtract(0, 0)
-        x3_g = interleave("x3", nc.vector.tensor_copy, x_raw[3][:])
+        x3_g = interleave("x3_g", x_raw[LAST], on_vector)
         copy_z2(0, 2)
         subtract(0, 1)
         copy_z2(0, 3)
@@ -158,143 +164,125 @@ def tile_rows_fsoftprod_kernel(tc, x, w1, w2, gn, hs, wo2, res, out):
         subtract(0, 2)
         subtract(0, 3)
         tanh(0, 0, G)
-        first_products(3, xq3)
-        exps(3, 0, 2 * C)
-        units = [(u, g) for u in (1, 2) for g in range(G)]
-        copy_z2(*units[0])
-        copy_z2(*units[1])
-        for k, (u, g) in enumerate(units):
-            subtract(u, g)
-            if u == 1 and g % 2 == 1:
-                tanh(1, g - 1, g + 1)
-            if k + 2 < len(units):
-                copy_z2(*units[k + 2])
-        tanh(2, 0, 3)
-        tanh(2, 3, G)
-
-        half = new("half", [P, G], F32)
-        nc.vector.tensor_scalar(out=half[:], in0=hscale[:], scalar1=0.5, scalar2=None, op0=ALU.mult)
-        wo_g = interleave("wo", nc.vector.tensor_copy, wo_raw[:])
-        gate = new("gate", [P, G, N], F32)
+        first_products(LAST, xq3, both_weights)
+        exps(LAST, BOTH)
+        exp_z_rt = new("exp_z_rt", [P, PACK, 2 * C], F32)
         for g in range(G):
-            nc.vector.tensor_scalar(
-                out=gate[:, g, :], in0=th[:, g, :], scalar1=1.0, scalar2=half[:, g : g + 1],
-                op0=ALU.add, op1=ALU.mult,
-            )
-            if g == 0:
-                woq = quantize("wo", wo_g)
+            move_to_row_tile(exp_z_rt, exp_z[LAST], g)
 
+        steps = [(s, g) for s in (1, 2) for g in range(G)]
+        copy_z2(*steps[0])
+        copy_z2(*steps[1])
+        for k, (s, g) in enumerate(steps):
+            subtract(s, g)
+            if s == 1 and g % 2 == 1:
+                tanh(s, g - 1, g + 1)
+            if k + 2 < len(steps):
+                copy_z2(*steps[k + 2])
+        tanh(2, 0, G - 1)
+        tanh(2, G - 1, G)
+
+        half_hs = new("half_hs", [P, G], F32)
+        nc.vector.tensor_scalar(out=half_hs[:], in0=hscale[:], scalar1=0.5, scalar2=None, op0=ALU.mult)
+        wo_g = interleave("wo_g", wo_raw, on_vector)
+
+        def gates(s):
+            dst = new("gate%d" % s, list(tanh_half[s].shape), F32)
+            for g in range(G):
+                nc.vector.tensor_scalar(
+                    out=dst[:, g, :], in0=tanh_half[s][:, g, :], scalar1=1.0, scalar2=half_hs[:, g : g + 1],
+                    op0=ALU.add, op1=ALU.mult,
+                )
+            return dst
+
+        gate_middle = gates(1)
+        gate_last = gates(2)
+        gate_rt = new("gate_rt", [P, PACK, C], F32)
+        for g in range(G):
+            move_to_row_tile(gate_rt, gate_last, g)
+        woq = quantize("wo", wo_g)
+        gate_first = gates(0)
+
+        ln_in = exp_z[:LAST] + [exp_z_rt]
+        gate = [gate_first[:], gate_middle[:, :, 0:C], gate_middle[:, :, C : 2 * C], gate_rt[:]]
+        gain_of = [gain] * LAST + [gain_rt]
         soft = [new("soft%d" % c, [P, G, 2 * C], F32) for c in range(CHUNKS)]
         prod = [new("prod%d" % c, [P, G, C], F32) for c in range(CHUNKS)]
         logp = [new("logp%d" % c, [P, G, C], F32) for c in range(CHUNKS)]
         hh = [new("hh%d" % c, [P, G, C], BF16) for c in range(CHUNKS)]
-        moved = [new("moved%d" % c, [P, PACK, C], BF16) for c in range(CHUNKS)]
+        hh_rt = [new("hh_rt%d" % c, [P, PACK, C], BF16) for c in range(LAST)] + [hh[LAST]]
         result = [new("result%d" % c, [P, G, C], F32) for c in range(CHUNKS)]
 
-        parts = [(c, slice(g, g + 2)) for c in range(CHUNKS) for g in (0, 2)][:-1]
-        parts = parts + [(CHUNKS - 1, slice(g, g + 1)) for g in (2, 3)]
-
-        def part(k):
-            return parts[k]
+        parts = [(c, slice(u, u + 2)) for c in range(CHUNKS) for u in (0, 2)][:-1]
+        parts = parts + [(LAST, slice(u, u + 1)) for u in (2, 3)]
 
         def softplus(k):
-            c, gs = part(k)
-            nc.scalar.activation(out=soft[c][:, gs, :], in_=e[c][:, gs, :], func=ACT.Ln, bias=1.0)
+            c, slots = parts[k]
+            nc.scalar.activation(out=soft[c][:, slots, :], in_=ln_in[c][:, slots, :], func=ACT.Ln, bias=1.0)
 
-        def products(k):
-            c, gs = part(k)
-            for g in range(gs.start, gs.stop):
+        def multiply(k):
+            c, slots = parts[k]
+            for u in range(slots.start, slots.stop):
                 nc.vector.scalar_tensor_tensor(
-                    out=prod[c][:, g, :], in0=soft[c][:, g, 0:C], scalar=gain[:, g : g + 1],
-                    in1=soft[c][:, g, C : 2 * C], op0=ALU.mult, op1=ALU.mult,
+                    out=prod[c][:, u, :], in0=soft[c][:, u, Z1], scalar=gain_of[c][:, u : u + 1],
+                    in1=soft[c][:, u, Z2], op0=ALU.mult, op1=ALU.mult,
                 )
-
-        def logs(k):
-            c, gs = part(k)
-            nc.scalar.activation(out=logp[c][:, gs, :], in_=prod[c][:, gs, :], func=ACT.Ln, bias=1.0)
 
         def hidden(k):
-            c, gs = part(k)
-            nc.vector.tensor_tensor(
-                out=hh[c][:, gs, :], in0=logp[c][:, gs, :], in1=gate[:, gs, c * C : (c + 1) * C], op=ALU.mult
-            )
-            for g in range(gs.start, gs.stop):
-                nc.sync.dma_start(out=moved[c][rows_of(g), :, :], in_=hh[c][:, g, :])
+            c, slots = parts[k]
+            nc.scalar.activation(out=logp[c][:, slots, :], in_=prod[c][:, slots, :], func=ACT.Ln, bias=1.0)
+            nc.vector.tensor_tensor(out=hh[c][:, slots, :], in0=logp[c][:, slots, :], in1=gate[c][:, slots, :], op=ALU.mult)
+            if c < LAST:
+                for g in range(slots.start, slots.stop):
+                    move_to_row_tile(hh_rt[c], hh[c], g)
 
         def y_of(g, c):
-            return banks[g][c % 2][:, 0:C]
+            col = (c // 2) * C
+            return bank_of(g, c)[:, col : col + C]
 
         def second_products(c, grouped):
-            hq = quantize("h%d" % c, grouped)
+            hq = quantize("hh%d" % c, grouped)
             for g in range(G):
-                product(y_of(g, c), g, woq, hq, 0)
+                product(y_of(g, c), g, woq, hq)
 
-        def finish(c, g0, g1, store_from):
+        def finish(c, g0):
             cols = slice(c * C, (c + 1) * C)
-            for g in range(g0, g1):
+            pair = slice(g0, g0 + 2)
+            for g in range(pair.start, pair.stop):
                 nc.vector.tensor_tensor(out=result[c][:, g, :], in0=y_of(g, c), in1=residual[:, g, cols], op=ALU.add)
-            if store_from is not None:
-                gs = slice(store_from, g1)
-                nc.sync.dma_start(out=out[gs, :, cols].rearrange("g o n -> o g n"), in_=result[c][:, gs, :])
+            nc.sync.dma_start(out=out[pair, :, cols].rearrange("g o n -> o g n"), in_=result[c][:, pair, :])
 
-        def interleave_shared(name, raw, split):
-            grouped = new(name + "_grouped", [P, C, PACK], BF16)
-            for copy, cols in ((nc.scalar.copy, slice(0, split)), (nc.vector.tensor_copy, slice(split, C))):
-                copy(
-                    out=grouped[:, cols, :].rearrange("p (c i) j -> p c j i", i=RUN),
-                    in_=raw[:, :, cols].rearrange("p j (c i) -> p c j i", i=RUN),
-                )
-            return grouped
+        LEAD = 3
+        singles = len(parts) - 2
+        for k in range(LEAD):
+            softplus(k)
+            multiply(k)
+        for k in range(LEAD - 1):
+            hidden(k)
+        for k in range(LEAD, singles):
+            softplus(k)
+            if k == singles - 1:
+                hh0_g = interleave("hh0_g", hh_rt[0], on_vector)
+            multiply(k)
+            hidden(k - 1)
+        softplus(singles)
+        second_products(0, hh0_g)
+        multiply(singles)
+        softplus(singles + 1)
+        multiply(singles + 1)
+        for k in range(singles - 1, len(parts)):
+            hidden(k)
 
-        softplus(0)
-        products(0)
-        softplus(1)
-        products(1)
-        logs(0)
-        hidden(0)
-        softplus(2)
-        products(2)
-        logs(1)
-        hidden(1)
-        softplus(3)
-        products(3)
-        logs(2)
-        hidden(2)
-        softplus(4)
-        products(4)
-        logs(3)
-        hidden(3)
-        softplus(5)
-        products(5)
-        logs(4)
-        hidden(4)
-        softplus(6)
-        h0 = interleave("h0", nc.vector.tensor_copy, moved[0][:])
-        products(6)
-        softplus(7)
-        products(7)
-        logs(5)
-        softplus(8)
-        hidden(5)
-        products(8)
-        logs(6)
-        second_products(0, h0)
-        hidden(6)
-        logs(7)
-        hidden(7)
-        logs(8)
-        hidden(8)
-        h1 = interleave("h1", nc.scalar.copy, moved[1][:])
-        finish(0, 0, 2, None)
-        second_products(1, h1)
-        finish(0, 2, G, 0)
-        finish(1, 0, 2, None)
-        h2 = interleave("h2", nc.vector.tensor_copy, moved[2][:])
-        finish(1, 2, G, 0)
-        second_products(2, h2)
-        h3 = interleave_shared("h3", moved[3], 48)
-        second_products(3, h3)
-        finish(2, 0, 2, 0)
-        finish(2, 2, G, 2)
-        finish(3, 0, 2, 0)
-        finish(3, 2, G, 2)
+        hh1_g = interleave("hh1_g", hh_rt[1], on_scalar)
+        hh3_g = interleave("hh3_g", hh_rt[LAST], on_scalar)
+        finish(0, 0)
+        second_products(1, hh1_g)
+        finish(0, 2)
+        hh2_g = interleave("hh2_g", hh_rt[2], on_scalar)
+        second_products(LAST, hh3_g)
+        finish(1, 0)
+        finish(1, 2)
+        second_products(2, hh2_g)
+        for c in (LAST, 2):
+            finish(c, 0)
+            finish(c, 2)

@@ -179,8 +179,9 @@ def tile_rows_fsoftprod_kernel(tc, x, w1, w2, gn, hs, wo2, res, out):
                 tanh(s, g - 1, g + 1)
             if k + 2 < len(steps):
                 copy_z2(*steps[k + 2])
-        tanh(2, 0, G - 1)
-        tanh(2, G - 1, G)
+        tanh(2, 0, 2)
+        tanh(2, 2, 3)
+        tanh(2, 3, G)
 
         half_hs = new("half_hs", [P, G], F32)
         nc.vector.tensor_scalar(out=half_hs[:], in0=hscale[:], scalar1=0.5, scalar2=None, op0=ALU.mult)
@@ -253,24 +254,22 @@ def tile_rows_fsoftprod_kernel(tc, x, w1, w2, gn, hs, wo2, res, out):
             nc.sync.dma_start(out=out[pair, :, cols].rearrange("g o n -> o g n"), in_=result[c][:, pair, :])
 
         LEAD = 3
-        singles = len(parts) - 2
+        first_single = len(parts) - 2
         for k in range(LEAD):
             softplus(k)
             multiply(k)
         for k in range(LEAD - 1):
             hidden(k)
-        for k in range(LEAD, singles):
+        for k in range(LEAD, first_single):
             softplus(k)
-            if k == singles - 1:
-                hh0_g = interleave("hh0_g", hh_rt[0], on_vector)
             multiply(k)
             hidden(k - 1)
-        softplus(singles)
+        hh0_g = interleave("hh0_g", hh_rt[0], on_vector)
+        for k in range(first_single, len(parts)):
+            softplus(k)
+            multiply(k)
         second_products(0, hh0_g)
-        multiply(singles)
-        softplus(singles + 1)
-        multiply(singles + 1)
-        for k in range(singles - 1, len(parts)):
+        for k in range(first_single - 1, len(parts)):
             hidden(k)
 
         hh1_g = interleave("hh1_g", hh_rt[1], on_scalar)

from contextlib import ExitStack

import concourse.mybir as mybir

G, D, M, O, N = 4, 128, 128, 128, 512
FLOPS = 2 * G * N * (2 * D * M + M * O)

F32 = mybir.dt.float32
BF16 = mybir.dt.bfloat16
U32 = mybir.dt.uint32
U8 = mybir.dt.uint8
FP8X4 = mybir.dt.float8_e4m3fn_x4
ACT = mybir.ActivationFunctionType
ALU = mybir.AluOpType

P = 128
PACK = 4
ROWS = P // G
C = 128
CHUNKS = N // C
LAST = CHUNKS - 1
RUN = 4
SCALAR_COLS = 48


def tile_rows_fsoftprod_kernel(tc, x, w1, w2, gn, hs, wo2, res, out):
    nc = tc.nc
    with ExitStack() as ctx:
        sb = ctx.enter_context(tc.tile_pool(name="sb", bufs=1))
        ps = ctx.enter_context(tc.psum_pool(name="ps", bufs=1))
        ctx.enter_context(tc.manual_schedule())

        def new(name, shape, dtype):
            return sb.tile(shape, dtype, name=name, align_bytes=64)

        def rows_of(g):
            return slice(ROWS * g, ROWS * (g + 1))

        def load_by_row_tile(name, src):
            raw = new(name, [P, PACK, src.shape[2]], F32)
            nc.sync.dma_start(out=raw[:], in_=src.rearrange("g (p j) n -> (g p) j n", j=PACK))
            return raw

        def move_to_row_tile(dst, src, g):
            nc.sync.dma_start(out=dst[rows_of(g), :, :], in_=src[:, g, :])

        def interleave(name, raw, shares):
            grouped = new(name, [P, C, PACK], BF16)
            for copy, cols in shares:
                copy(
                    out=grouped[:, cols, :].rearrange("p (c i) j -> p c j i", i=RUN),
                    in_=raw[:, :, cols].rearrange("p j (c i) -> p c j i", i=RUN),
                )
            return grouped

        on_vector = [(nc.vector.tensor_copy, slice(0, C))]
        on_scalar = [(nc.scalar.copy, slice(0, C))]
        on_both = [(nc.scalar.copy, slice(0, SCALAR_COLS)), (nc.vector.tensor_copy, slice(SCALAR_COLS, C))]

        def quantize(name, grouped):
            codes = new(name + "_codes", [P, C], U32)
            scales = new(name + "_scales", [P, C], U8)
            nc.vector.quantize_mx(
                out=codes[:].bitcast(FP8X4),
                scales=scales[:],
                in_=grouped[:].rearrange("p n j -> p (n j)"),
            )
            return codes, scales

        def product(dst, g, weights, moving):
            r = rows_of(g)
            nc.tensor.matmul_mx(
                out=dst,
                lhsT=weights[0][r, :].bitcast(FP8X4),
                lhsT_scale=weights[1][r, :],
                rhs=moving[0][r, :].bitcast(FP8X4),
                rhs_scale=moving[1][r, :],
                start=True,
                stop=True,
            )

        x_raw = [load_by_row_tile("x0_raw", x[:, :, 0:C])]
        w1_raw = load_by_row_tile("w1_raw", w1)
        w2_raw = load_by_row_tile("w2_raw", w2)
        for c in range(1, CHUNKS):
            x_raw.append(load_by_row_tile("x%d_raw" % c, x[:, :, c * C : (c + 1) * C]))
        wo_raw = load_by_row_tile("wo_raw", wo2)
        hscale = new("hscale", [P, G], F32)
        gain = new("gain", [P, G], F32)
        with nc.allow_non_contiguous_dma(reason="one value for each partition and group"):
            nc.sync.dma_start(out=hscale[:], in_=hs.rearrange("g m o -> m (g o)"))
            nc.sync.dma_start(out=gain[:], in_=gn.rearrange("g m o -> m (g o)"))
        gain_rt = new("gain_rt", [P, PACK], F32)
        nc.sync.dma_start(out=gain_rt[:], in_=gn.rearrange("g (p j) o -> (g p) (j o)", j=PACK))
        residual = new("residual", [P, G, N], F32)
        nc.sync.dma_start(out=residual[:], in_=res.rearrange("g o n -> o g n"))

        banks = [[ps.tile([P, 4 * C], F32, name="bank%d_%d" % (g, b)) for b in range(2)] for g in range(G)]

        def bank_of(g, c):
            return banks[g][1 if 0 < c < LAST else 0]

        spans = [(0, 1), (1, LAST), (LAST, CHUNKS)]

        def z_of(g, c0, c1):
            col = (c0 // 2) * 2 * C
            return bank_of(g, c0)[:, col : col + (c1 - c0) * 2 * C].rearrange("p (c n) -> p c n", n=2 * C)

        exp_z = [new("exp_z%d" % c, [P, G, 2 * C], F32) for c in range(CHUNKS)]
        z2 = [new("z2_%d" % s, [P, G, c1 - c0, C], F32) for s, (c0, c1) in enumerate(spans)]
        diff = [new("diff%d" % s, [P, G, c1 - c0, C], F32) for s, (c0, c1) in enumerate(spans)]
        tanh_half = [new("tanh_half%d" % s, [P, G, (c1 - c0) * C], F32) for s, (c0, c1) in enumerate(spans)]
        Z1, Z2, BOTH = slice(0, C), slice(C, 2 * C), slice(0, 2 * C)

        def first_products(c, xq, which):
            for g in range(G):
                for weights, cols in which:
                    product(z_of(g, c, c + 1)[:, 0, cols], g, weights, xq)

        def exps(c, cols):
            for g in range(G):
                nc.scalar.activation(out=exp_z[c][:, g, cols], in_=z_of(g, c, c + 1)[:, 0, cols], func=ACT.Exp)

        def copy_z2(s, g):
            nc.vector.tensor_copy(out=z2[s][:, g], in_=z_of(g, *spans[s])[:, :, Z2])

        def subtract(s, g):
            nc.vector.tensor_tensor(out=diff[s][:, g], in0=z_of(g, *spans[s])[:, :, Z1], in1=z2[s][:, g], op=ALU.subtract)

        def tanh(s, g0, g1):
            nc.scalar.activation(
                out=tanh_half[s][:, g0:g1, :],
                in_=diff[s][:, g0:g1].rearrange("p g c n -> p g (c n)"),
                func=ACT.Tanh,
                scale=0.5,
            )

        x0_g = interleave("x0_g", x_raw[0], on_vector)
        w1_g = interleave("w1_g", w1_raw, on_both)
        xq0 = quantize("x0", x0_g)
        w1q = quantize("w1", w1_g)
        first_products(0, xq0, [(w1q, Z1)])
        w2_g = interleave("w2_g", w2_raw, on_both)
        exps(0, Z1)
        w2q = quantize("w2", w2_g)
        first_products(0, xq0, [(w2q, Z2)])
        both_weights = [(w1q, Z1), (w2q, Z2)]
        x1_g = interleave("x1_g", x_raw[1], on_vector)
        exps(0, Z2)
        first_products(1, quantize("x1", x1_g), both_weights)

        x2_g = interleave("x2_g", x_raw[2], on_vector)
        exps(1, BOTH)
        copy_z2(0, 0)
        first_products(2, quantize("x2", x2_g), both_weights)
        exps(2, BOTH)
        copy_z2(0, 1)
        subtract(0, 0)
        x3_g = interleave("x3_g", x_raw[LAST], on_vector)
        copy_z2(0, 2)
        subtract(0, 1)
        copy_z2(0, 3)
        xq3 = quantize("x3", x3_g)
        subtract(0, 2)
        subtract(0, 3)
        tanh(0, 0, G)
        first_products(LAST, xq3, both_weights)
        exps(LAST, BOTH)
        exp_z_rt = new("exp_z_rt", [P, PACK, 2 * C], F32)
        for g in range(G):
            move_to_row_tile(exp_z_rt, exp_z[LAST], g)

        steps = [(s, g) for s in (1, 2) for g in range(G)]
        copy_z2(*steps[0])
        copy_z2(*steps[1])
        for k, (s, g) in enumerate(steps):
            subtract(s, g)
            if s == 1 and g % 2 == 1:
                tanh(s, g - 1, g + 1)
            if k + 2 < len(steps):
                copy_z2(*steps[k + 2])
        tanh(2, 0, 2)
        tanh(2, 2, 3)
        tanh(2, 3, G)

        half_hs = new("half_hs", [P, G], F32)
        nc.vector.tensor_scalar(out=half_hs[:], in0=hscale[:], scalar1=0.5, scalar2=None, op0=ALU.mult)
        wo_g = interleave("wo_g", wo_raw, on_vector)

        def gates(s):
            dst = new("gate%d" % s, list(tanh_half[s].shape), F32)
            for g in range(G):
                nc.vector.tensor_scalar(
                    out=dst[:, g, :], in0=tanh_half[s][:, g, :], scalar1=1.0, scalar2=half_hs[:, g : g + 1],
                    op0=ALU.add, op1=ALU.mult,
                )
            return dst

        gate_middle = gates(1)
        gate_last = gates(2)
        gate_rt = new("gate_rt", [P, PACK, C], F32)
        for g in range(G):
            move_to_row_tile(gate_rt, gate_last, g)
        woq = quantize("wo", wo_g)
        gate_first = gates(0)

        ln_in = exp_z[:LAST] + [exp_z_rt]
        gate = [gate_first[:], gate_middle[:, :, 0:C], gate_middle[:, :, C : 2 * C], gate_rt[:]]
        gain_of = [gain] * LAST + [gain_rt]
        soft = [new("soft%d" % c, [P, G, 2 * C], F32) for c in range(CHUNKS)]
        prod = [new("prod%d" % c, [P, G, C], F32) for c in range(CHUNKS)]
        logp = [new("logp%d" % c, [P, G, C], F32) for c in range(CHUNKS)]
        hh = [new("hh%d" % c, [P, G, C], BF16) for c in range(CHUNKS)]
        hh_rt = [new("hh_rt%d" % c, [P, PACK, C], BF16) for c in range(LAST)] + [hh[LAST]]
        result = [new("result%d" % c, [P, G, C], F32) for c in range(CHUNKS)]

        parts = [(c, slice(u, u + 2)) for c in range(CHUNKS) for u in (0, 2)][:-1]
        parts = parts + [(LAST, slice(u, u + 1)) for u in (2, 3)]

        def softplus(k):
            c, slots = parts[k]
            nc.scalar.activation(out=soft[c][:, slots, :], in_=ln_in[c][:, slots, :], func=ACT.Ln, bias=1.0)

        def multiply(k):
            c, slots = parts[k]
            for u in range(slots.start, slots.stop):
                nc.vector.scalar_tensor_tensor(
                    out=prod[c][:, u, :], in0=soft[c][:, u, Z1], scalar=gain_of[c][:, u : u + 1],
                    in1=soft[c][:, u, Z2], op0=ALU.mult, op1=ALU.mult,
                )

        def hidden(k):
            c, slots = parts[k]
            nc.scalar.activation(out=logp[c][:, slots, :], in_=prod[c][:, slots, :], func=ACT.Ln, bias=1.0)
            nc.vector.tensor_tensor(out=hh[c][:, slots, :], in0=logp[c][:, slots, :], in1=gate[c][:, slots, :], op=ALU.mult)
            if c < LAST:
                for g in range(slots.start, slots.stop):
                    move_to_row_tile(hh_rt[c], hh[c], g)

        def y_of(g, c):
            col = (c // 2) * C
            return bank_of(g, c)[:, col : col + C]

        def second_products(c, grouped):
            hq = quantize("hh%d" % c, grouped)
            for g in range(G):
                product(y_of(g, c), g, woq, hq)

        def finish(c, g0):
            cols = slice(c * C, (c + 1) * C)
            pair = slice(g0, g0 + 2)
            for g in range(pair.start, pair.stop):
                nc.vector.tensor_tensor(out=result[c][:, g, :], in0=y_of(g, c), in1=residual[:, g, cols], op=ALU.add)
            nc.sync.dma_start(out=out[pair, :, cols].rearrange("g o n -> o g n"), in_=result[c][:, pair, :])

        LEAD = 3
        first_single = len(parts) - 2
        for k in range(LEAD):
            softplus(k)
            multiply(k)
        for k in range(LEAD - 1):
            hidden(k)
        for k in range(LEAD, first_single):
            softplus(k)
            multiply(k)
            hidden(k - 1)
        hh0_g = interleave("hh0_g", hh_rt[0], on_vector)
        for k in range(first_single, len(parts)):
            softplus(k)
            multiply(k)
        second_products(0, hh0_g)
        for k in range(first_single - 1, len(parts)):
            hidden(k)

        hh1_g = interleave("hh1_g", hh_rt[1], on_scalar)
        hh3_g = interleave("hh3_g", hh_rt[LAST], on_scalar)
        finish(0, 0)
        second_products(1, hh1_g)
        finish(0, 2)
        hh2_g = interleave("hh2_g", hh_rt[2], on_scalar)
        second_products(LAST, hh3_g)
        finish(1, 0)
        finish(1, 2)
        second_products(2, hh2_g)
        for c in (LAST, 2):
            finish(c, 0)
            finish(c, 2)
